import numpy as np
import ml_dtypes


def mxq(x, axis, fmt="e4m3"):
    dtype, down = {"e4m3": (ml_dtypes.float8_e4m3fn, 7), "e5m2": (ml_dtypes.float8_e5m2, 14)}[fmt]
    v = np.moveaxis(np.asarray(x, np.float32).astype(ml_dtypes.bfloat16).astype(np.float64), axis, -1)
    blocks = v.reshape(v.shape[:-1] + (-1, 32))
    amax = np.abs(blocks).max(-1, keepdims=True)
    byte = np.maximum(np.where(amax > 0, np.frexp(amax)[1] - 1 + 127, 0) - down, 1)
    scale = np.exp2(byte - 127.0)
    codes = (blocks / scale).astype(np.float32).astype(dtype).astype(np.float64)
    return np.moveaxis((codes * scale).reshape(v.shape), -1, axis)


WIDE = False


def mx_kscale(k):
    if not WIDE:
        return np.ones(k)
    levels = np.array([10, -10, 5, -5, 0])
    if k % 512:
        return np.exp2(np.random.permutation(np.resize(levels, k // 32))).repeat(32)
    a = np.empty((k // 512, 16))
    for p in range(k // 512):
        a[p, :8] = np.random.permutation(np.resize(levels, 8))
        for g in range(8):
            far = levels[np.abs(levels - a[p, g]) >= 10]
            a[p, g + 8] = far[np.random.randint(len(far))]
    return np.exp2(a.ravel()).repeat(32)


def f64(x):
    return np.asarray(x).astype(np.float64)


def striped(idx):
    return np.tile(np.asarray(idx).reshape(-1, 16).T, (8, 1)).astype(np.uint16)


def unstriped(offs):
    return offs[:16].T.reshape(-1).astype(np.int64)


B, N, T, D, DV, NQ = 1, 512, 1024, 512, 256, 256
NEW = 128


def setup_inputs():
    n = np.random.standard_normal
    idx = np.random.permutation(T)[:B * N]
    s = mx_kscale(D)[:, None]
    u = np.ones(T)
    u[idx] = mx_kscale(B * N)
    r = np.random.uniform(0.5, 2.0, T)
    k = n((D, T)) / s
    v = n((DV, T)) / (u * r)
    new = np.random.permutation(idx.reshape(B, N)[:, -NEW // B:].reshape(-1))
    return {
        "qT": (n((B, D, NQ)) * s * (0.80 / np.sqrt(D))).astype(np.float32),
        "kT": np.where(np.isin(np.arange(T), new)[None, :], n((D, T)), k).astype(np.float32),
        "vT": np.where(np.isin(np.arange(T), new)[None, :], n((DV, T)), v).astype(np.float32),
        "new_kT": k[:, new].astype(np.float32),
        "new_vT": v[:, new].astype(np.float32),
        "vs": np.tile(u * r, (128, 1)).astype(np.float32),
        "og": n((B, NQ, DV)).astype(np.float32),
        "offs": striped(idx),
        "slots": striped(new),
    }


def reference(qT, kT, vT, new_kT, new_vT, vs, og, offs, slots):
    idx = unstriped(offs)
    k = f64(kT)
    k[:, unstriped(slots)] = f64(new_kT)
    v = f64(vT)
    v[:, unstriped(slots)] = f64(new_vT)
    pick = lambda x: x[:, idx].reshape(x.shape[0], B, N).transpose(1, 0, 2)
    q = f64(qT)
    score = mxq(q, 1, "e4m3").transpose(0, 2, 1) @ mxq(pick(k), 1, "e4m3")
    m = score.max(-1, keepdims=True)
    p = np.exp(score - m)
    total = p.sum(-1, keepdims=True)
    w = p * pick(f64(vs))[:, :1, :]
    y = mxq(w, 2, "e4m3") @ mxq(pick(v).transpose(0, 2, 1), 1, "e4m3")
    y = y / total
    y = y / (1.0 + np.exp(-f64(og)))
    return y

@@ -1,0 +1,160 @@
+from contextlib import ExitStack
+
+import concourse.mybir as mybir
+from concourse.masks import make_identity
+
+F32 = mybir.dt.float32
+BF16 = mybir.dt.bfloat16
+U32 = mybir.dt.uint32
+U16 = mybir.dt.uint16
+U8 = mybir.dt.uint8
+FP8X4 = mybir.dt.float8_e4m3fn_x4
+ACT = mybir.ActivationFunctionType
+ALU = mybir.AluOpType
+AXX = mybir.AxisListType.X
+
+D, DV, T, N, NQ, NEW = 512, 256, 1024, 512, 256, 128
+P = 128
+PACK = 4
+QT = NQ // P
+ET = DV // P
+
+FLOPS = 2 * NQ * N * (D + DV)
+
+
+def tile_attend_x_append128_gate_topk_kernel(tc, qT, kT, vT, new_kT, new_vT, vs, og, offs, slots, out):
+    nc = tc.nc
+    with ExitStack() as ctx:
+        keep = ctx.enter_context(tc.tile_pool(name="keep", bufs=1))
+        psum = ctx.enter_context(tc.psum_pool(name="psum", bufs=1))
+
+        slots_t = keep.tile([P, NEW // 16], U16, name="slots_t")
+        offs_t = keep.tile([P, N // 16], U16, name="offs_t")
+        newk = keep.tile([P, PACK, NEW], F32, name="newk")
+        newv = keep.tile([P, ET, NEW], F32, name="newv")
+        kp = [keep.tile([P, T], F32, name=f"kp{t}") for t in range(PACK)]
+        vp = [keep.tile([P, T], F32, name=f"vp{h}") for h in range(ET)]
+        qf = keep.tile([P, PACK, NQ], F32, name="qf")
+        vs_t = keep.tile([P, T], F32, name="vs_t")
+        og_t = keep.tile([P, QT, DV], F32, name="og_t")
+
+        kview = kT.rearrange("(p t) n -> p t n", t=PACK)
+        vview = vT.rearrange("(h p) n -> p h n", p=P)
+        nc.sync.dma_start(slots_t[:], slots)
+        nc.sync.dma_start(newk[:], new_kT.rearrange("(p t) n -> p t n", t=PACK))
+        nc.sync.dma_start(kp[0][:], kview[:, 0, :])
+        nc.sync.dma_start(offs_t[:], offs)
+        nc.sync.dma_start(kp[1][:], kview[:, 1, :])
+        nc.sync.dma_start(kp[2][:], kview[:, 2, :])
+        nc.sync.dma_start(kp[3][:], kview[:, 3, :])
+        nc.sync.dma_start(qf[:], qT[0].rearrange("(p t) n -> p t n", t=PACK))
+        nc.sync.dma_start(newv[:], new_vT.rearrange("(h p) n -> p h n", p=P))
+        nc.sync.dma_start(vp[0][:], vview[:, 0, :])
+        nc.sync.dma_start(vp[1][:], vview[:, 1, :])
+        nc.sync.dma_start(vs_t[:], vs)
+        nc.sync.dma_start(og_t[:], og[0].rearrange("(a p) e -> p a e", p=P))
+
+        warm = keep.tile([P, 1], F32, name="warm")
+        nc.vector.memset(warm[:], 0.0)
+        warm_out = keep.tile([P, 1], F32, name="warm_out")
+        nc.scalar.activation(warm_out[:], warm[:], ACT.Exp)
+
+        ident_f = keep.tile([P, P], F32, name="ident_f")
+        make_identity(nc, ident_f[:])
+        ident_b = keep.tile([P, P], BF16, name="ident_b")
+        make_identity(nc, ident_b[:])
+
+        ki = keep.tile([P, N, PACK], BF16, name="ki", align_bytes=64)
+        for t in range(PACK):
+            nc.vector.tensor_copy(kp[t][:].indirect(slots_t[:]), newk[:, t, :])
+            if t < 2:
+                kb = keep.tile([P, T], BF16, name=f"kb{t}")
+                nc.scalar.activation(kb[:], kp[t][:], ACT.Copy)
+                nc.scalar.activation(ki[:, :, t], kb[:].indirect(offs_t[:]), ACT.Copy)
+            else:
+                nc.vector.tensor_copy(ki[:, :, t], kp[t][:].indirect(offs_t[:]))
+
+        qi = keep.tile([P, NQ, PACK], BF16, name="qi", align_bytes=64)
+        nc.scalar.activation(qi[:], qf[:].rearrange("p t n -> p n t"), ACT.Copy)
+        qc = keep.tile([P, NQ], U32, name="qc", align_bytes=64)
+        qs = keep.tile([P, NQ], U8, name="qs", align_bytes=64)
+        nc.vector.quantize_mx(out=qc[:].bitcast(FP8X4), scales=qs[:], in_=qi[:].rearrange("p n t -> p (n t)"))
+        kc = keep.tile([P, N], U32, name="kc", align_bytes=64)
+        ks = keep.tile([P, N], U8, name="ks", align_bytes=64)
+        nc.vector.quantize_mx(out=kc[:].bitcast(FP8X4), scales=ks[:], in_=ki[:].rearrange("p n t -> p (n t)"))
+
+        sc = []
+        for a in range(QT):
+            cols = slice(a * P, (a + 1) * P)
+            s_ps = psum.tile([P, N], F32, name=f"s_ps{a}")
+            nc.tensor.matmul_mx(s_ps[:], lhsT=qc[:, cols].bitcast(FP8X4), lhsT_scale=qs[:, cols],
+                                rhs=kc[:].bitcast(FP8X4), rhs_scale=ks[:], start=True, stop=True)
+            sc.append(s_ps)
+
+        vg = keep.tile([P, ET, PACK, P], BF16, name="vg")
+        for h in range(ET):
+            nc.vector.tensor_copy(vp[h][:].indirect(slots_t[:]), newv[:, h, :])
+        negm = []
+        for a in range(QT):
+            nm = keep.tile([P, 1], F32, name=f"nm{a}")
+            nc.vector.tensor_reduce(nm[:], sc[a][:], axis=AXX, op=ALU.max, negate=True)
+            negm.append(nm)
+        for h in range(ET):
+            nc.vector.tensor_copy(vg[:, h].rearrange("p t s -> p s t"), vp[h][:].indirect(offs_t[:]))
+        vsg = keep.tile([P, N], F32, name="vsg")
+        nc.vector.tensor_copy(vsg[:], vs_t[:].indirect(offs_t[:]))
+
+        p_t = []
+        l_t = []
+        for a in range(QT):
+            pt = keep.tile([P, PACK, P], F32, name=f"pt{a}")
+            lt = keep.tile([P, 1], F32, name=f"lt{a}")
+            nc.scalar.activation(pt[:], sc[a][:].rearrange("q (s t) -> q t s", t=PACK), ACT.Exp,
+                                 bias=negm[a][:], scale=1.0, accum_out=lt[:])
+            p_t.append(pt)
+            l_t.append(lt)
+
+        vs_ps = psum.tile([P, PACK, P], F32, name="vs_ps")
+        for t in range(PACK):
+            nc.tensor.transpose(vs_ps[:, t, :], vsg[:].rearrange("p (s t) -> p t s", t=PACK)[:, t, :], ident_f[:])
+        vsc = keep.tile([P, PACK], F32, name="vsc")
+        nc.scalar.copy(vsc[:], vs_ps[:, :, 0])
+
+        wi = []
+        for a in range(QT):
+            w_ps = psum.tile([P, PACK, P], F32, name=f"w_ps{a}")
+            for t in range(PACK):
+                nc.tensor.transpose(w_ps[:, t, :], p_t[a][:, t, :], ident_f[:])
+            w_i = keep.tile([P, P, PACK], BF16, name=f"w_i{a}", align_bytes=64)
+            nc.vector.tensor_tensor(w_i[:], w_ps[:].rearrange("s t q -> s q t"),
+                                    vsc[:].unsqueeze(1).to_broadcast([P, P, PACK]), ALU.mult)
+            wi.append(w_i)
+
+        v_ps = psum.tile([P, PACK, DV], BF16, name="v_ps")
+        for h in range(ET):
+            for t in range(PACK):
+                nc.tensor.transpose(v_ps[:, t, h * P : (h + 1) * P], vg[:, h, t, :], ident_b[:])
+        vi = keep.tile([P, DV, PACK], BF16, name="vi", align_bytes=64)
+        nc.scalar.copy(vi[:], v_ps[:].rearrange("s t e -> s e t"))
+        vc = keep.tile([P, DV], U32, name="vc", align_bytes=64)
+        vsx = keep.tile([P, DV], U8, name="vsx", align_bytes=64)
+        nc.vector.quantize_mx(out=vc[:].bitcast(FP8X4), scales=vsx[:], in_=vi[:].rearrange("p n t -> p (n t)"))
+
+        th = keep.tile([P, QT, DV], F32, name="th")
+        nc.scalar.activation(th[:], og_t[:], ACT.Tanh, scale=0.5)
+        gate = keep.tile([P, QT, DV], F32, name="gate")
+        nc.gpsimd.tensor_scalar(gate[:], th[:], 0.5, 0.5, ALU.mult, ALU.add)
+
+        oview = out[0].rearrange("(a p) e -> a p e", p=P)
+        for a in range(QT):
+            rl = keep.tile([P, 1], F32, name=f"rl{a}")
+            nc.vector.reciprocal(rl[:], l_t[a][:])
+            wc = keep.tile([P, P], U32, name=f"wc{a}", align_bytes=64)
+            ws = keep.tile([P, P], U8, name=f"ws{a}", align_bytes=64)
+            nc.vector.quantize_mx(out=wc[:].bitcast(FP8X4), scales=ws[:], in_=wi[a][:].rearrange("p n t -> p (n t)"))
+            y_ps = psum.tile([P, DV], F32, name=f"y_ps{a}")
+            nc.tensor.matmul_mx(y_ps[:], lhsT=wc[:].bitcast(FP8X4), lhsT_scale=ws[:],
+                                rhs=vc[:].bitcast(FP8X4), rhs_scale=vsx[:], start=True, stop=True)
+            res = keep.tile([P, DV], F32, name=f"res{a}")
+            nc.vector.scalar_tensor_tensor(res[:], y_ps[:], rl[:], gate[:, a, :], ALU.mult, ALU.mult)
+            nc.sync.dma_start(oview[a], res[:])

@@ -27,134 +27,122 @@ def tile_attend_x_append128_gate_topk_kernel(tc, qT, kT, vT, new_kT, new_vT, vs,
     with ExitStack() as ctx:
         keep = ctx.enter_context(tc.tile_pool(name="keep", bufs=1))
         psum = ctx.enter_context(tc.psum_pool(name="psum", bufs=1))
-
         slots_t = keep.tile([P, NEW // 16], U16, name="slots_t")
         offs_t = keep.tile([P, N // 16], U16, name="offs_t")
-        newk = keep.tile([P, PACK, NEW], F32, name="newk")
-        newv = keep.tile([P, ET, NEW], F32, name="newv")
         kp = [keep.tile([P, T], F32, name=f"kp{t}") for t in range(PACK)]
+        kb = [keep.tile([P, T], BF16, name=f"kb{t}") for t in range(PACK)]
         vp = [keep.tile([P, T], F32, name=f"vp{h}") for h in range(ET)]
+        vb = [keep.tile([P, T], BF16, name=f"vb{h}") for h in range(ET)]
+        newk = keep.tile([P, PACK, NEW], F32, name="newk")
+        newka = keep.tile([P, 1, NEW], F32, name="newka")
+        newkb = keep.tile([P, 3, NEW], F32, name="newkb")
+        newv = keep.tile([P, ET, NEW], F32, name="newv")
         qf = keep.tile([P, PACK, NQ], F32, name="qf")
         vs_t = keep.tile([P, T], F32, name="vs_t")
         og_t = keep.tile([P, QT, DV], F32, name="og_t")
-
+        ki = keep.tile([P, N, PACK], BF16, name="ki", align_bytes=64)
+        g2t = keep.tile([P, 2, N], F32, name="g2t")
+        qi = keep.tile([P, NQ, PACK], BF16, name="qi", align_bytes=64)
+        qc = keep.tile([P, NQ], U32, name="qc", align_bytes=64)
+        qs = keep.tile([P, NQ], U8, name="qs", align_bytes=64)
+        kc = keep.tile([P, N], U32, name="kc", align_bytes=64)
+        ks = keep.tile([P, N], U8, name="ks", align_bytes=64)
+        vg = [keep.tile([P, PACK, P], BF16, name=f"vg{h}") for h in range(ET)]
+        vsg = keep.tile([P, N], F32, name="vsg")
+        vsc = keep.tile([P, PACK], F32, name="vsc")
+        vi = keep.tile([P, DV, PACK], BF16, name="vi", align_bytes=64)
+        vc = keep.tile([P, DV], U32, name="vc", align_bytes=64)
+        vsx = keep.tile([P, DV], U8, name="vsx", align_bytes=64)
+        th = keep.tile([P, QT, DV], F32, name="th")
+        gate = keep.tile([P, QT, DV], F32, name="gate")
+        nm = [keep.tile([P, 1], F32, name=f"nm{a}") for a in range(QT)]
+        lt = [keep.tile([P, 1], F32, name=f"lt{a}") for a in range(QT)]
+        rl = [keep.tile([P, 1], F32, name=f"rl{a}") for a in range(QT)]
+        pt = [keep.tile([P, PACK, P], F32, name=f"pt{a}") for a in range(QT)]
+        wi = [keep.tile([P, P, PACK], BF16, name=f"wi{a}", align_bytes=64) for a in range(QT)]
+        wc = [keep.tile([P, P], U32, name=f"wc{a}", align_bytes=64) for a in range(QT)]
+        ws = [keep.tile([P, P], U8, name=f"ws{a}", align_bytes=64) for a in range(QT)]
+        res = [keep.tile([P, DV], F32, name=f"res{a}") for a in range(QT)]
+        s_ps = [psum.tile([P, N], F32, name=f"s_ps{a}") for a in range(QT)]
+        w_ps = [psum.tile([P, PACK, P], F32, name=f"w_ps{a}") for a in range(QT)]
+        y_ps = [psum.tile([P, DV], F32, name=f"y_ps{a}") for a in range(QT)]
+        vs_ps = psum.tile([P, PACK, P], F32, name="vs_ps")
+        v_ps = psum.tile([P, PACK, DV], BF16, name="v_ps")
         kview = kT.rearrange("(p t) n -> p t n", t=PACK)
+        nkview = new_kT.rearrange("(p t) n -> p t n", t=PACK)
         vview = vT.rearrange("(h p) n -> p h n", p=P)
+        oview = out[0].rearrange("(a p) e -> a p e", p=P)
         nc.sync.dma_start(slots_t[:], slots)
-        nc.sync.dma_start(newk[:], new_kT.rearrange("(p t) n -> p t n", t=PACK))
-        nc.sync.dma_start(kp[0][:], kview[:, 0, :])
-        nc.sync.dma_start(offs_t[:], offs)
+        nc.sync.dma_start(newk[:], nkview)
         nc.sync.dma_start(kp[1][:], kview[:, 1, :])
+        nc.sync.dma_start(kp[0][:], kview[:, 0, :])
         nc.sync.dma_start(kp[2][:], kview[:, 2, :])
         nc.sync.dma_start(kp[3][:], kview[:, 3, :])
-        nc.sync.dma_start(qf[:], qT[0].rearrange("(p t) n -> p t n", t=PACK))
+        nc.sync.dma_start(offs_t[:], offs)
         nc.sync.dma_start(newv[:], new_vT.rearrange("(h p) n -> p h n", p=P))
+        nc.sync.dma_start(qf[:], qT[0].rearrange("(p t) n -> p t n", t=PACK))
         nc.sync.dma_start(vp[0][:], vview[:, 0, :])
-        nc.sync.dma_start(vp[1][:], vview[:, 1, :])
-        nc.sync.dma_start(vs_t[:], vs)
         nc.sync.dma_start(og_t[:], og[0].rearrange("(a p) e -> p a e", p=P))
-
+        nc.sync.dma_start(vs_t[:], vs)
+        nc.sync.dma_start(vp[1][:], vview[:, 1, :])
         warm = keep.tile([P, 1], F32, name="warm")
         nc.vector.memset(warm[:], 0.0)
         warm_out = keep.tile([P, 1], F32, name="warm_out")
         nc.scalar.activation(warm_out[:], warm[:], ACT.Exp)
-
         ident_f = keep.tile([P, P], F32, name="ident_f")
         make_identity(nc, ident_f[:])
         ident_b = keep.tile([P, P], BF16, name="ident_b")
         make_identity(nc, ident_b[:])
-
-        ki = keep.tile([P, N, PACK], BF16, name="ki", align_bytes=64)
-        for t in range(PACK):
-            nc.vector.tensor_copy(kp[t][:].indirect(slots_t[:]), newk[:, t, :])
-            if t < 2:
-                kb = keep.tile([P, T], BF16, name=f"kb{t}")
-                nc.scalar.activation(kb[:], kp[t][:], ACT.Copy)
-                nc.scalar.activation(ki[:, :, t], kb[:].indirect(offs_t[:]), ACT.Copy)
-            else:
-                nc.vector.tensor_copy(ki[:, :, t], kp[t][:].indirect(offs_t[:]))
-
-        qi = keep.tile([P, NQ, PACK], BF16, name="qi", align_bytes=64)
+        nc.vector.tensor_copy(kp[2][:].indirect(slots_t[:]), newk[:, 2, :])
+        nc.vector.tensor_copy(kp[1][:].indirect(slots_t[:]), newk[:, 1, :])
+        nc.vector.tensor_copy(kp[0][:].indirect(slots_t[:]), newk[:, 0, :])
+        nc.vector.tensor_copy(vp[0][:].indirect(slots_t[:]), newv[:, 0, :])
+        nc.scalar.activation(kb[1][:], kp[1][:], ACT.Copy)
         nc.scalar.activation(qi[:], qf[:].rearrange("p t n -> p n t"), ACT.Copy)
-        qc = keep.tile([P, NQ], U32, name="qc", align_bytes=64)
-        qs = keep.tile([P, NQ], U8, name="qs", align_bytes=64)
-        nc.vector.quantize_mx(out=qc[:].bitcast(FP8X4), scales=qs[:], in_=qi[:].rearrange("p n t -> p (n t)"))
-        kc = keep.tile([P, N], U32, name="kc", align_bytes=64)
-        ks = keep.tile([P, N], U8, name="ks", align_bytes=64)
+        nc.vector.tensor_copy(kp[3][:].indirect(slots_t[:]), newk[:, 3, :])
+        nc.scalar.activation(ki[:, :, 1], kb[1][:].indirect(offs_t[:]), ACT.Copy)
+        nc.scalar.activation(kb[0][:], kp[0][:], ACT.Copy)
+        nc.vector.tensor_copy(ki[:, :, 2], kp[2][:].indirect(offs_t[:]))
+        nc.scalar.activation(ki[:, :, 0], kb[0][:].indirect(offs_t[:]), ACT.Copy)
+        nc.scalar.activation(vb[0][:], vp[0][:], ACT.Copy)
+        nc.scalar.activation(vg[0][:].rearrange("p t s -> p s t"), vb[0][:].indirect(offs_t[:]), ACT.Copy)
+        for t in range(PACK):
+            nc.tensor.transpose(v_ps[:, t, 0:128], vg[0][:, t, :], ident_b[:])
+        nc.vector.tensor_copy(ki[:, :, 3], kp[3][:].indirect(offs_t[:]))
         nc.vector.quantize_mx(out=kc[:].bitcast(FP8X4), scales=ks[:], in_=ki[:].rearrange("p n t -> p (n t)"))
-
-        sc = []
-        for a in range(QT):
-            cols = slice(a * P, (a + 1) * P)
-            s_ps = psum.tile([P, N], F32, name=f"s_ps{a}")
-            nc.tensor.matmul_mx(s_ps[:], lhsT=qc[:, cols].bitcast(FP8X4), lhsT_scale=qs[:, cols],
-                                rhs=kc[:].bitcast(FP8X4), rhs_scale=ks[:], start=True, stop=True)
-            sc.append(s_ps)
-
-        vg = keep.tile([P, ET, PACK, P], BF16, name="vg")
-        for h in range(ET):
-            nc.vector.tensor_copy(vp[h][:].indirect(slots_t[:]), newv[:, h, :])
-        negm = []
-        for a in range(QT):
-            nm = keep.tile([P, 1], F32, name=f"nm{a}")
-            nc.vector.tensor_reduce(nm[:], sc[a][:], axis=AXX, op=ALU.max, negate=True)
-            negm.append(nm)
-        for h in range(ET):
-            nc.vector.tensor_copy(vg[:, h].rearrange("p t s -> p s t"), vp[h][:].indirect(offs_t[:]))
-        vsg = keep.tile([P, N], F32, name="vsg")
         nc.vector.tensor_copy(vsg[:], vs_t[:].indirect(offs_t[:]))
-
-        p_t = []
-        l_t = []
-        for a in range(QT):
-            pt = keep.tile([P, PACK, P], F32, name=f"pt{a}")
-            lt = keep.tile([P, 1], F32, name=f"lt{a}")
-            nc.scalar.activation(pt[:], sc[a][:].rearrange("q (s t) -> q t s", t=PACK), ACT.Exp,
-                                 bias=negm[a][:], scale=1.0, accum_out=lt[:])
-            p_t.append(pt)
-            l_t.append(lt)
-
-        vs_ps = psum.tile([P, PACK, P], F32, name="vs_ps")
         for t in range(PACK):
             nc.tensor.transpose(vs_ps[:, t, :], vsg[:].rearrange("p (s t) -> p t s", t=PACK)[:, t, :], ident_f[:])
-        vsc = keep.tile([P, PACK], F32, name="vsc")
+        nc.vector.quantize_mx(out=qc[:].bitcast(FP8X4), scales=qs[:], in_=qi[:].rearrange("p n t -> p (n t)"))
         nc.scalar.copy(vsc[:], vs_ps[:, :, 0])
-
-        wi = []
-        for a in range(QT):
-            w_ps = psum.tile([P, PACK, P], F32, name=f"w_ps{a}")
-            for t in range(PACK):
-                nc.tensor.transpose(w_ps[:, t, :], p_t[a][:, t, :], ident_f[:])
-            w_i = keep.tile([P, P, PACK], BF16, name=f"w_i{a}", align_bytes=64)
-            nc.vector.tensor_tensor(w_i[:], w_ps[:].rearrange("s t q -> s q t"),
-                                    vsc[:].unsqueeze(1).to_broadcast([P, P, PACK]), ALU.mult)
-            wi.append(w_i)
-
-        v_ps = psum.tile([P, PACK, DV], BF16, name="v_ps")
-        for h in range(ET):
-            for t in range(PACK):
-                nc.tensor.transpose(v_ps[:, t, h * P : (h + 1) * P], vg[:, h, t, :], ident_b[:])
-        vi = keep.tile([P, DV, PACK], BF16, name="vi", align_bytes=64)
-        nc.scalar.copy(vi[:], v_ps[:].rearrange("s t e -> s e t"))
-        vc = keep.tile([P, DV], U32, name="vc", align_bytes=64)
-        vsx = keep.tile([P, DV], U8, name="vsx", align_bytes=64)
-        nc.vector.quantize_mx(out=vc[:].bitcast(FP8X4), scales=vsx[:], in_=vi[:].rearrange("p n t -> p (n t)"))
-
-        th = keep.tile([P, QT, DV], F32, name="th")
         nc.scalar.activation(th[:], og_t[:], ACT.Tanh, scale=0.5)
-        gate = keep.tile([P, QT, DV], F32, name="gate")
+        nc.tensor.matmul_mx(s_ps[0][:], lhsT=qc[:, 0:128].bitcast(FP8X4), lhsT_scale=qs[:, 0:128], rhs=kc[:].bitcast(FP8X4), rhs_scale=ks[:], start=True, stop=True)
         nc.gpsimd.tensor_scalar(gate[:], th[:], 0.5, 0.5, ALU.mult, ALU.add)
-
-        oview = out[0].rearrange("(a p) e -> a p e", p=P)
-        for a in range(QT):
-            rl = keep.tile([P, 1], F32, name=f"rl{a}")
-            nc.vector.reciprocal(rl[:], l_t[a][:])
-            wc = keep.tile([P, P], U32, name=f"wc{a}", align_bytes=64)
-            ws = keep.tile([P, P], U8, name=f"ws{a}", align_bytes=64)
-            nc.vector.quantize_mx(out=wc[:].bitcast(FP8X4), scales=ws[:], in_=wi[a][:].rearrange("p n t -> p (n t)"))
-            y_ps = psum.tile([P, DV], F32, name=f"y_ps{a}")
-            nc.tensor.matmul_mx(y_ps[:], lhsT=wc[:].bitcast(FP8X4), lhsT_scale=ws[:],
-                                rhs=vc[:].bitcast(FP8X4), rhs_scale=vsx[:], start=True, stop=True)
-            res = keep.tile([P, DV], F32, name=f"res{a}")
-            nc.vector.scalar_tensor_tensor(res[:], y_ps[:], rl[:], gate[:, a, :], ALU.mult, ALU.mult)
-            nc.sync.dma_start(oview[a], res[:])
+        nc.scalar.copy(vi[:, 0:128, :], v_ps[:, :, 0:128].rearrange("s t e -> s e t"))
+        nc.tensor.matmul_mx(s_ps[1][:], lhsT=qc[:, 128:256].bitcast(FP8X4), lhsT_scale=qs[:, 128:256], rhs=kc[:].bitcast(FP8X4), rhs_scale=ks[:], start=True, stop=True)
+        nc.vector.tensor_reduce(nm[1][:], s_ps[1][:], axis=AXX, op=ALU.max, negate=True)
+        nc.vector.tensor_copy(vp[1][:].indirect(slots_t[:]), newv[:, 1, :])
+        nc.vector.tensor_copy(vg[1][:].rearrange("p t s -> p s t"), vp[1][:].indirect(offs_t[:]))
+        for t in range(PACK):
+            nc.tensor.transpose(v_ps[:, t, 128:256], vg[1][:, t, :], ident_b[:])
+        nc.vector.tensor_reduce(nm[0][:], s_ps[0][:], axis=AXX, op=ALU.max, negate=True)
+        nc.scalar.copy(vi[:, 128:256, :], v_ps[:, :, 128:256].rearrange("s t e -> s e t"))
+        nc.scalar.activation(pt[1][:], s_ps[1][:].rearrange("q (s t) -> q t s", t=PACK), ACT.Exp, bias=nm[1][:], scale=1.0, accum_out=lt[1][:])
+        for t in range(PACK):
+            nc.tensor.transpose(w_ps[1][:, t, :], pt[1][:, t, :], ident_f[:])
+        nc.vector.tensor_tensor(wi[1][:], w_ps[1][:].rearrange("s t q -> s q t"), vsc[:].unsqueeze(1).to_broadcast([P, P, PACK]), ALU.mult)
+        nc.vector.quantize_mx(out=wc[1][:].bitcast(FP8X4), scales=ws[1][:], in_=wi[1][:].rearrange("p n t -> p (n t)"))
+        nc.scalar.activation(pt[0][:], s_ps[0][:].rearrange("q (s t) -> q t s", t=PACK), ACT.Exp, bias=nm[0][:], scale=1.0, accum_out=lt[0][:])
+        nc.vector.reciprocal(rl[0][:], lt[0][:])
+        for t in range(PACK):
+            nc.tensor.transpose(w_ps[0][:, t, :], pt[0][:, t, :], ident_f[:])
+        nc.vector.tensor_tensor(wi[0][:], w_ps[0][:].rearrange("s t q -> s q t"), vsc[:].unsqueeze(1).to_broadcast([P, P, PACK]), ALU.mult)
+        nc.vector.quantize_mx(out=vc[:].bitcast(FP8X4), scales=vsx[:], in_=vi[:].rearrange("p n t -> p (n t)"))
+        nc.tensor.matmul_mx(y_ps[1][:], lhsT=wc[1][:].bitcast(FP8X4), lhsT_scale=ws[1][:], rhs=vc[:].bitcast(FP8X4), rhs_scale=vsx[:], start=True, stop=True)
+        nc.vector.quantize_mx(out=wc[0][:].bitcast(FP8X4), scales=ws[0][:], in_=wi[0][:].rearrange("p n t -> p (n t)"))
+        nc.tensor.matmul_mx(y_ps[0][:], lhsT=wc[0][:].bitcast(FP8X4), lhsT_scale=ws[0][:], rhs=vc[:].bitcast(FP8X4), rhs_scale=vsx[:], start=True, stop=True)
+        nc.vector.reciprocal(rl[1][:], lt[1][:])
+        nc.vector.scalar_tensor_tensor(res[1][:], y_ps[1][:], rl[1][:], gate[:, 1, :], ALU.mult, ALU.mult)
+        nc.sync.dma_start(oview[1], res[1][:])
+        nc.vector.scalar_tensor_tensor(res[0][:], y_ps[0][:], rl[0][:], gate[:, 0, :], ALU.mult, ALU.mult)
+        nc.sync.dma_start(oview[0], res[0][:])

@@ -56,8 +56,8 @@ def tile_attend_x_append128_gate_topk_kernel(tc, qT, kT, vT, new_kT, new_vT, vs,
         th = keep.tile([P, QT, DV], F32, name="th")
         gate = keep.tile([P, QT, DV], F32, name="gate")
         nm = [keep.tile([P, 1], F32, name=f"nm{a}") for a in range(QT)]
-        lt = [keep.tile([P, 1], F32, name=f"lt{a}") for a in range(QT)]
-        rl = [keep.tile([P, 1], F32, name=f"rl{a}") for a in range(QT)]
+        lt = keep.tile([P, QT], F32, name="lt")
+        rl = keep.tile([P, QT], F32, name="rl")
         pt = [keep.tile([P, PACK, P], F32, name=f"pt{a}") for a in range(QT)]
         wi = [keep.tile([P, P, PACK], BF16, name=f"wi{a}", align_bytes=64) for a in range(QT)]
         wc = [keep.tile([P, P], U32, name=f"wc{a}", align_bytes=64) for a in range(QT)]
@@ -86,7 +86,7 @@ def tile_attend_x_append128_gate_topk_kernel(tc, qT, kT, vT, new_kT, new_vT, vs,
         nc.sync.dma_start(vs_t[:], vs)
         nc.sync.dma_start(vp[1][:], vview[:, 1, :])
         warm = keep.tile([P, 1], F32, name="warm")
-        nc.vector.memset(warm[:], 0.0)
+        nc.gpsimd.memset(warm[:], 0.0)
         warm_out = keep.tile([P, 1], F32, name="warm_out")
         nc.scalar.activation(warm_out[:], warm[:], ACT.Exp)
         ident_f = keep.tile([P, P], F32, name="ident_f")
@@ -98,7 +98,7 @@ def tile_attend_x_append128_gate_topk_kernel(tc, qT, kT, vT, new_kT, new_vT, vs,
         nc.vector.tensor_copy(kp[0][:].indirect(slots_t[:]), newk[:, 0, :])
         nc.vector.tensor_copy(vp[0][:].indirect(slots_t[:]), newv[:, 0, :])
         nc.scalar.activation(kb[1][:], kp[1][:], ACT.Copy)
-        nc.scalar.activation(qi[:], qf[:].rearrange("p t n -> p n t"), ACT.Copy)
+        nc.gpsimd.tensor_scalar(qi[:], qf[:].rearrange("p t n -> p n t"), 1.0, 0.0, ALU.mult, ALU.add)
         nc.vector.tensor_copy(kp[3][:].indirect(slots_t[:]), newk[:, 3, :])
         nc.scalar.activation(ki[:, :, 1], kb[1][:].indirect(offs_t[:]), ACT.Copy)
         nc.scalar.activation(kb[0][:], kp[0][:], ACT.Copy)
@@ -127,13 +127,13 @@ def tile_attend_x_append128_gate_topk_kernel(tc, qT, kT, vT, new_kT, new_vT, vs,
             nc.tensor.transpose(v_ps[:, t, 128:256], vg[1][:, t, :], ident_b[:])
         nc.vector.tensor_reduce(nm[0][:], s_ps[0][:], axis=AXX, op=ALU.max, negate=True)
         nc.scalar.copy(vi[:, 128:256, :], v_ps[:, :, 128:256].rearrange("s t e -> s e t"))
-        nc.scalar.activation(pt[1][:], s_ps[1][:].rearrange("q (s t) -> q t s", t=PACK), ACT.Exp, bias=nm[1][:], scale=1.0, accum_out=lt[1][:])
+        nc.scalar.activation(pt[1][:], s_ps[1][:].rearrange("q (s t) -> q t s", t=PACK), ACT.Exp, bias=nm[1][:], scale=1.0, accum_out=lt[:, 1:2])
         for t in range(PACK):
             nc.tensor.transpose(w_ps[1][:, t, :], pt[1][:, t, :], ident_f[:])
         nc.vector.tensor_tensor(wi[1][:], w_ps[1][:].rearrange("s t q -> s q t"), vsc[:].unsqueeze(1).to_broadcast([P, P, PACK]), ALU.mult)
         nc.vector.quantize_mx(out=wc[1][:].bitcast(FP8X4), scales=ws[1][:], in_=wi[1][:].rearrange("p n t -> p (n t)"))
-        nc.scalar.activation(pt[0][:], s_ps[0][:].rearrange("q (s t) -> q t s", t=PACK), ACT.Exp, bias=nm[0][:], scale=1.0, accum_out=lt[0][:])
-        nc.vector.reciprocal(rl[0][:], lt[0][:])
+        nc.scalar.activation(pt[0][:], s_ps[0][:].rearrange("q (s t) -> q t s", t=PACK), ACT.Exp, bias=nm[0][:], scale=1.0, accum_out=lt[:, 0:1])
+        nc.vector.reciprocal(rl[:], lt[:])
         for t in range(PACK):
             nc.tensor.transpose(w_ps[0][:, t, :], pt[0][:, t, :], ident_f[:])
         nc.vector.tensor_tensor(wi[0][:], w_ps[0][:].rearrange("s t q -> s q t"), vsc[:].unsqueeze(1).to_broadcast([P, P, PACK]), ALU.mult)
@@ -141,8 +141,7 @@ def tile_attend_x_append128_gate_topk_kernel(tc, qT, kT, vT, new_kT, new_vT, vs,
         nc.tensor.matmul_mx(y_ps[1][:], lhsT=wc[1][:].bitcast(FP8X4), lhsT_scale=ws[1][:], rhs=vc[:].bitcast(FP8X4), rhs_scale=vsx[:], start=True, stop=True)
         nc.vector.quantize_mx(out=wc[0][:].bitcast(FP8X4), scales=ws[0][:], in_=wi[0][:].rearrange("p n t -> p (n t)"))
         nc.tensor.matmul_mx(y_ps[0][:], lhsT=wc[0][:].bitcast(FP8X4), lhsT_scale=ws[0][:], rhs=vc[:].bitcast(FP8X4), rhs_scale=vsx[:], start=True, stop=True)
-        nc.vector.reciprocal(rl[1][:], lt[1][:])
-        nc.vector.scalar_tensor_tensor(res[1][:], y_ps[1][:], rl[1][:], gate[:, 1, :], ALU.mult, ALU.mult)
+        nc.vector.scalar_tensor_tensor(res[1][:], y_ps[1][:], rl[:, 1:2], gate[:, 1, :], ALU.mult, ALU.mult)
         nc.sync.dma_start(oview[1], res[1][:])
-        nc.vector.scalar_tensor_tensor(res[0][:], y_ps[0][:], rl[0][:], gate[:, 0, :], ALU.mult, ALU.mult)
+        nc.vector.scalar_tensor_tensor(res[0][:], y_ps[0][:], rl[:, 0:1], gate[:, 0, :], ALU.mult, ALU.mult)
         nc.sync.dma_start(oview[0], res[0][:])

from contextlib import ExitStack

import concourse.mybir as mybir
from concourse.masks import make_identity

F32 = mybir.dt.float32
BF16 = mybir.dt.bfloat16
U32 = mybir.dt.uint32
U16 = mybir.dt.uint16
U8 = mybir.dt.uint8
FP8X4 = mybir.dt.float8_e4m3fn_x4
ACT = mybir.ActivationFunctionType
ALU = mybir.AluOpType
AXX = mybir.AxisListType.X

D, DV, T, N, NQ, NEW = 512, 256, 1024, 512, 256, 128
P = 128
PACK = 4
QT = NQ // P
ET = DV // P

FLOPS = 2 * NQ * N * (D + DV)


def tile_attend_x_append128_gate_topk_kernel(tc, qT, kT, vT, new_kT, new_vT, vs, og, offs, slots, out):
    nc = tc.nc
    with ExitStack() as ctx:
        keep = ctx.enter_context(tc.tile_pool(name="keep", bufs=1))
        psum = ctx.enter_context(tc.psum_pool(name="psum", bufs=1))
        slots_t = keep.tile([P, NEW // 16], U16, name="slots_t")
        offs_t = keep.tile([P, N // 16], U16, name="offs_t")
        kp = [keep.tile([P, T], F32, name=f"kp{t}") for t in range(PACK)]
        kb = [keep.tile([P, T], BF16, name=f"kb{t}") for t in range(PACK)]
        vp = [keep.tile([P, T], F32, name=f"vp{h}") for h in range(ET)]
        vb = [keep.tile([P, T], BF16, name=f"vb{h}") for h in range(ET)]
        newk = keep.tile([P, PACK, NEW], F32, name="newk")
        newka = keep.tile([P, 1, NEW], F32, name="newka")
        newkb = keep.tile([P, 3, NEW], F32, name="newkb")
        newv = keep.tile([P, ET, NEW], F32, name="newv")
        qf = keep.tile([P, PACK, NQ], F32, name="qf")
        vs_t = keep.tile([P, T], F32, name="vs_t")
        og_t = keep.tile([P, QT, DV], F32, name="og_t")
        ki = keep.tile([P, N, PACK], BF16, name="ki", align_bytes=64)
        g2t = keep.tile([P, 2, N], F32, name="g2t")
        qi = keep.tile([P, NQ, PACK], BF16, name="qi", align_bytes=64)
        qc = keep.tile([P, NQ], U32, name="qc", align_bytes=64)
        qs = keep.tile([P, NQ], U8, name="qs", align_bytes=64)
        kc = keep.tile([P, N], U32, name="kc", align_bytes=64)
        ks = keep.tile([P, N], U8, name="ks", align_bytes=64)
        vg = [keep.tile([P, PACK, P], BF16, name=f"vg{h}") for h in range(ET)]
        vsg = keep.tile([P, N], F32, name="vsg")
        vsc = keep.tile([P, PACK], F32, name="vsc")
        vi = keep.tile([P, DV, PACK], BF16, name="vi", align_bytes=64)
        vc = keep.tile([P, DV], U32, name="vc", align_bytes=64)
        vsx = keep.tile([P, DV], U8, name="vsx", align_bytes=64)
        th = keep.tile([P, QT, DV], F32, name="th")
        gate = keep.tile([P, QT, DV], F32, name="gate")
        nm = [keep.tile([P, 1], F32, name=f"nm{a}") for a in range(QT)]
        lt = keep.tile([P, QT], F32, name="lt")
        rl = keep.tile([P, QT], F32, name="rl")
        pt = [keep.tile([P, PACK, P], F32, name=f"pt{a}") for a in range(QT)]
        wi = [keep.tile([P, P, PACK], BF16, name=f"wi{a}", align_bytes=64) for a in range(QT)]
        wc = [keep.tile([P, P], U32, name=f"wc{a}", align_bytes=64) for a in range(QT)]
        ws = [keep.tile([P, P], U8, name=f"ws{a}", align_bytes=64) for a in range(QT)]
        res = [keep.tile([P, DV], F32, name=f"res{a}") for a in range(QT)]
        s_ps = [psum.tile([P, N], F32, name=f"s_ps{a}") for a in range(QT)]
        w_ps = [psum.tile([P, PACK, P], F32, name=f"w_ps{a}") for a in range(QT)]
        y_ps = [psum.tile([P, DV], F32, name=f"y_ps{a}") for a in range(QT)]
        vs_ps = psum.tile([P, PACK, P], F32, name="vs_ps")
        v_ps = psum.tile([P, PACK, DV], BF16, name="v_ps")
        kview = kT.rearrange("(p t) n -> p t n", t=PACK)
        nkview = new_kT.rearrange("(p t) n -> p t n", t=PACK)
        vview = vT.rearrange("(h p) n -> p h n", p=P)
        oview = out[0].rearrange("(a p) e -> a p e", p=P)
        nc.sync.dma_start(slots_t[:], slots)
        nc.sync.dma_start(newk[:], nkview)
        nc.sync.dma_start(kp[1][:], kview[:, 1, :])
        nc.sync.dma_start(kp[0][:], kview[:, 0, :])
        nc.sync.dma_start(kp[2][:], kview[:, 2, :])
        nc.sync.dma_start(kp[3][:], kview[:, 3, :])
        nc.sync.dma_start(offs_t[:], offs)
        nc.sync.dma_start(newv[:], new_vT.rearrange("(h p) n -> p h n", p=P))
        nc.sync.dma_start(qf[:], qT[0].rearrange("(p t) n -> p t n", t=PACK))
        nc.sync.dma_start(vp[0][:], vview[:, 0, :])
        nc.sync.dma_start(og_t[:], og[0].rearrange("(a p) e -> p a e", p=P))
        nc.sync.dma_start(vs_t[:], vs)
        nc.sync.dma_start(vp[1][:], vview[:, 1, :])
        warm = keep.tile([P, 1], F32, name="warm")
        nc.gpsimd.memset(warm[:], 0.0)
        warm_out = keep.tile([P, 1], F32, name="warm_out")
        nc.scalar.activation(warm_out[:], warm[:], ACT.Exp)
        ident_f = keep.tile([P, P], F32, name="ident_f")
        make_identity(nc, ident_f[:])
        ident_b = keep.tile([P, P], BF16, name="ident_b")
        make_identity(nc, ident_b[:])
        nc.vector.tensor_copy(kp[2][:].indirect(slots_t[:]), newk[:, 2, :])
        nc.vector.tensor_copy(kp[1][:].indirect(slots_t[:]), newk[:, 1, :])
        nc.vector.tensor_copy(kp[0][:].indirect(slots_t[:]), newk[:, 0, :])
        nc.vector.tensor_copy(vp[0][:].indirect(slots_t[:]), newv[:, 0, :])
        nc.scalar.activation(kb[1][:], kp[1][:], ACT.Copy)
        nc.gpsimd.tensor_scalar(qi[:], qf[:].rearrange("p t n -> p n t"), 1.0, 0.0, ALU.mult, ALU.add)
        nc.vector.tensor_copy(kp[3][:].indirect(slots_t[:]), newk[:, 3, :])
        nc.scalar.activation(ki[:, :, 1], kb[1][:].indirect(offs_t[:]), ACT.Copy)
        nc.scalar.activation(kb[0][:], kp[0][:], ACT.Copy)
        nc.vector.tensor_copy(ki[:, :, 2], kp[2][:].indirect(offs_t[:]))
        nc.scalar.activation(ki[:, :, 0], kb[0][:].indirect(offs_t[:]), ACT.Copy)
        nc.scalar.activation(vb[0][:], vp[0][:], ACT.Copy)
        nc.scalar.activation(vg[0][:].rearrange("p t s -> p s t"), vb[0][:].indirect(offs_t[:]), ACT.Copy)
        for t in range(PACK):
            nc.tensor.transpose(v_ps[:, t, 0:128], vg[0][:, t, :], ident_b[:])
        nc.vector.tensor_copy(ki[:, :, 3], kp[3][:].indirect(offs_t[:]))
        nc.vector.quantize_mx(out=kc[:].bitcast(FP8X4), scales=ks[:], in_=ki[:].rearrange("p n t -> p (n t)"))
        nc.vector.tensor_copy(vsg[:], vs_t[:].indirect(offs_t[:]))
        for t in range(PACK):
            nc.tensor.transpose(vs_ps[:, t, :], vsg[:].rearrange("p (s t) -> p t s", t=PACK)[:, t, :], ident_f[:])
        nc.vector.quantize_mx(out=qc[:].bitcast(FP8X4), scales=qs[:], in_=qi[:].rearrange("p n t -> p (n t)"))
        nc.scalar.copy(vsc[:], vs_ps[:, :, 0])
        nc.scalar.activation(th[:], og_t[:], ACT.Tanh, scale=0.5)
        nc.tensor.matmul_mx(s_ps[0][:], lhsT=qc[:, 0:128].bitcast(FP8X4), lhsT_scale=qs[:, 0:128], rhs=kc[:].bitcast(FP8X4), rhs_scale=ks[:], start=True, stop=True)
        nc.gpsimd.tensor_scalar(gate[:], th[:], 0.5, 0.5, ALU.mult, ALU.add)
        nc.scalar.copy(vi[:, 0:128, :], v_ps[:, :, 0:128].rearrange("s t e -> s e t"))
        nc.tensor.matmul_mx(s_ps[1][:], lhsT=qc[:, 128:256].bitcast(FP8X4), lhsT_scale=qs[:, 128:256], rhs=kc[:].bitcast(FP8X4), rhs_scale=ks[:], start=True, stop=True)
        nc.vector.tensor_reduce(nm[1][:], s_ps[1][:], axis=AXX, op=ALU.max, negate=True)
        nc.vector.tensor_copy(vp[1][:].indirect(slots_t[:]), newv[:, 1, :])
        nc.vector.tensor_copy(vg[1][:].rearrange("p t s -> p s t"), vp[1][:].indirect(offs_t[:]))
        for t in range(PACK):
            nc.tensor.transpose(v_ps[:, t, 128:256], vg[1][:, t, :], ident_b[:])
        nc.vector.tensor_reduce(nm[0][:], s_ps[0][:], axis=AXX, op=ALU.max, negate=True)
        nc.scalar.copy(vi[:, 128:256, :], v_ps[:, :, 128:256].rearrange("s t e -> s e t"))
        nc.scalar.activation(pt[1][:], s_ps[1][:].rearrange("q (s t) -> q t s", t=PACK), ACT.Exp, bias=nm[1][:], scale=1.0, accum_out=lt[:, 1:2])
        for t in range(PACK):
            nc.tensor.transpose(w_ps[1][:, t, :], pt[1][:, t, :], ident_f[:])
        nc.vector.tensor_tensor(wi[1][:], w_ps[1][:].rearrange("s t q -> s q t"), vsc[:].unsqueeze(1).to_broadcast([P, P, PACK]), ALU.mult)
        nc.vector.quantize_mx(out=wc[1][:].bitcast(FP8X4), scales=ws[1][:], in_=wi[1][:].rearrange("p n t -> p (n t)"))
        nc.scalar.activation(pt[0][:], s_ps[0][:].rearrange("q (s t) -> q t s", t=PACK), ACT.Exp, bias=nm[0][:], scale=1.0, accum_out=lt[:, 0:1])
        nc.vector.reciprocal(rl[:], lt[:])
        for t in range(PACK):
            nc.tensor.transpose(w_ps[0][:, t, :], pt[0][:, t, :], ident_f[:])
        nc.vector.tensor_tensor(wi[0][:], w_ps[0][:].rearrange("s t q -> s q t"), vsc[:].unsqueeze(1).to_broadcast([P, P, PACK]), ALU.mult)
        nc.vector.quantize_mx(out=vc[:].bitcast(FP8X4), scales=vsx[:], in_=vi[:].rearrange("p n t -> p (n t)"))
        nc.tensor.matmul_mx(y_ps[1][:], lhsT=wc[1][:].bitcast(FP8X4), lhsT_scale=ws[1][:], rhs=vc[:].bitcast(FP8X4), rhs_scale=vsx[:], start=True, stop=True)
        nc.vector.quantize_mx(out=wc[0][:].bitcast(FP8X4), scales=ws[0][:], in_=wi[0][:].rearrange("p n t -> p (n t)"))
        nc.tensor.matmul_mx(y_ps[0][:], lhsT=wc[0][:].bitcast(FP8X4), lhsT_scale=ws[0][:], rhs=vc[:].bitcast(FP8X4), rhs_scale=vsx[:], start=True, stop=True)
        nc.vector.scalar_tensor_tensor(res[1][:], y_ps[1][:], rl[:, 1:2], gate[:, 1, :], ALU.mult, ALU.mult)
        nc.sync.dma_start(oview[1], res[1][:])
        nc.vector.scalar_tensor_tensor(res[0][:], y_ps[0][:], rl[:, 0:1], gate[:, 0, :], ALU.mult, ALU.mult)
        nc.sync.dma_start(oview[0], res[0][:])
